import numpy as np, ml_dtypes
CORES = [51,54,179,182]
N = 4
import mx_ref
BF = ml_dtypes.bfloat16
def entries(a):
    return np.ascontiguousarray(a.T).reshape(-1)
def table(e):
    return np.ascontiguousarray(np.reshape(e, (-1, 16)).T).astype(np.int32)
def cols(t, e):
    v = np.concatenate([t.reshape(128, -1, 4), np.zeros((128, 1, 4), BF)], axis=1)
    return np.ascontiguousarray(v[:, e]).reshape(128, -1)
def cut(t, i, w=512):
    return t[:, w * i:w * i + w]
def f(rng, *shape):
    return mx_ref.flush((rng.standard_normal(shape, dtype=np.float32) * np.exp2(rng.integers(-2, 3, shape[:-1] + (1,)))).astype(BF))
def wide(rng, *shape, cols=0):
    v = rng.standard_normal(shape, dtype=np.float32) * np.exp2(rng.integers(-12, 13, shape)).astype(np.float32)
    if cols: v *= np.repeat(np.exp2(rng.integers(-cols, cols + 1, shape[:-2] + (1, shape[-1] // 4))) * (rng.random(shape[:-2] + (1, shape[-1] // 4)) > 0.0625), 4, axis=-1).astype(np.float32)
    return mx_ref.flush(v.astype(BF))
T, K, O, CAPP = 512, 8, 1, 96
def lists(rng, foreign=False, own=False, same=False, absent=False):
    S = np.full((N, N, CAPP), -1); M = []
    for s in range(N):
        for d in range(N):
            n = CAPP if foreign else rng.integers(1, CAPP + 1)
            if s != d: S[s, d, rng.permutation(CAPP)[:n]] = rng.integers(0, T, n)
    k = np.arange(K)[:, None]
    for r in range(N):
        far = T + np.flatnonzero(S[:, r].reshape(-1) >= 0)
        m = np.where(rng.random((K, T)) < (1.0 if foreign else np.divide(k + 1, K + 1)), rng.choice(far, (K, T)), rng.integers(0, T, (K, T)))
        there = np.zeros((K, T), bool); there[rng.integers(0, K, T), np.arange(T)] = True
        if absent: there.reshape(-1)[rng.permutation(np.flatnonzero(~there))[:K * T - 2 * K * T // 3 - T]] = True
        else: there |= rng.random((K, T)) >= 0.1 + 0.5 * np.divide(k, K - 1)
        m = np.repeat(m[:, :1], T, axis=1) if same else np.where(there, m, -1)
        if own: m = np.stack([rng.permutation(T) for _ in range(K)])
        M.append(table(m))
    return {"send": np.stack([table(S[s]) for s in range(N)]), "mp": np.stack(M)}
def setup_inputs(rng):
    return {"x": f(rng, N, 128, 4 * T), "w": f(rng, N, 128, K * O * 512), **lists(rng)}
def setup_inputs_absent(rng):
    return {**setup_inputs(rng), **lists(rng, absent=True)}
def setup_inputs_foreign(rng):
    return {**setup_inputs(rng), **lists(rng, foreign=True)}
def setup_inputs_same(rng):
    return {**setup_inputs(rng), **lists(rng, same=True)}
def setup_inputs_spread(rng):
    d = setup_inputs(rng); d["x"] = wide(rng, N, 128, 4 * T); return d
def setup_inputs_own(rng):
    return {**setup_inputs(rng), **lists(rng, own=True)}
def check_inputs(d):
    b = []
    for n in ("x", "w"):
        a = np.abs(d[n].astype(np.float32))
        if not np.isfinite(a).all() or ((a > 0) & ((a < 2.0 ** -30) | (a > 2.0 ** 30))).any(): b.append(n)
    for r in range(N):
        s, m = entries(d["send"][r]), entries(d["mp"][r]).reshape(K, T)
        if s.min() < -1 or s.max() >= T or (s[r * CAPP:(r + 1) * CAPP] != -1).any(): b.append("send")
        held = np.concatenate([entries(d["send"][q])[r * CAPP:(r + 1) * CAPP] for q in range(N)])
        if m.min() < -1 or m.max() >= T + N * CAPP or (held[m[m >= T] - T] < 0).any() or (m < 0).all(axis=0).any(): b.append("mp")
    return b
def reference(x, w, send, mp):
    y = np.zeros((N, 128, O * T), np.float32)
    for r in range(N):
        held = [cols(x[s], entries(send[s])[r * CAPP:(r + 1) * CAPP]) for s in range(N)]
        v = np.concatenate([x[r]] + held, axis=1)
        m = entries(mp[r]).reshape(K, T)
        for k in range(K):
            q = mx_ref.quantize(cols(v, m[k]))
            for o in range(O): y[r][:, T * o:T * o + T] += mx_ref.matmul(mx_ref.quantize(cut(w[r], k * O + o)), q)
    return {"y": y}

@@ -1,0 +1,241 @@
+from concourse.bass import DstId, RemoteDMATransfer
+from concourse.mybir import dt, AluOpType, ActivationFunctionType
+
+COLS, MAPS, CAPP, N = 512, 8, 96, 4
+SLOTS = (N - 1) * CAPP
+WIN = 1 + COLS + SLOTS
+NE = 8
+CUT = [(0, 128), (128, 448), (448, 512)]
+VM = [[2, 7], [1, 2, 3, 4, 6, 5, 7], [5, 7]]
+ORDER = {
+    "v": [("E", 0), ("E", 1), ("E", 2), ("P", 1, 1), ("P", 2, 1), ("P", 2, 0), ("P", 3, 1), ("P", 4, 1), ("P", 5, 2), ("P", 6, 1),
+          ("P", 5, 1), ("Z", 0), ("F", 1), ("Z", 2), ("F", 0), ("F", 2)],
+    "s": [("P", 0, 1), ("P", 1, 0), ("E", 3), ("E", 4), ("E", 5), ("E", 6), ("P", 0, 2), ("P", 6, 2), ("P", 4, 0), ("P", 5, 0),
+          ("P", 6, 0), ("P", 3, 0), ("P", 0, 0), ("P", 4, 2), ("P", 1, 2), ("P", 2, 2), ("E", 7), ("P", 3, 2)],
+}
+SM = [[x[1] for x in ORDER["s"] if x[0] == "P" and x[2] == j] for j in range(len(CUT))]
+VOWN = [2, 5]
+TERMS = 6
+
+SCRATCH = {
+    "xs": ("sbuf", [128, 4 * COLS], "bfloat16"),
+    "wt": ("sbuf", [128, 512 * MAPS], "bfloat16"),
+    "sl": ("sbuf", [32, N * CAPP // 16], "int32"),
+    "so": ("sbuf", [128, N * CAPP // 16], "uint16"),
+    "ml": ("sbuf", [128, MAPS * COLS // 16], "int32"),
+    "mt": ("sbuf", [128, MAPS * COLS // 16], "int32"),
+    "mu": ("sbuf", [128, MAPS * COLS // 16], "int32"),
+    "mo": ("sbuf", [128, MAPS * COLS // 16], "uint16"),
+    "h": ("sbuf", [128, 4 * SLOTS], "bfloat16"),
+    "hq": ("sbuf", [128, 2 * CAPP], "float8_e4m3fn_x4"),
+    "hs": ("sbuf", [128, 2 * CAPP], "uint8"),
+    "nq": ("sbuf", [128, 128], "float8_e4m3fn_x4"),
+    "ns": ("sbuf", [128, 128], "uint8"),
+    "qf": ("sbuf", [128, COLS + SLOTS], "float8_e4m3fn_x4"),
+    "sf": ("sbuf", [128, COLS + SLOTS], "uint8"),
+    "qw": ("sbuf", [128, 128 * MAPS], "float8_e4m3fn_x4"),
+    "sw": ("sbuf", [128, 128 * MAPS], "uint8"),
+    "win": ("sbuf", [128, MAPS * WIN], "float32"),
+    "gs": ("sbuf", [128, 2 * COLS], "float32"),
+    "vs": ("sbuf", [128, MAPS * COLS], "float32"),
+    "pq": ("sbuf", [128, TERMS * COLS], "float32"),
+    "zz": ("sbuf", [128, TERMS * COLS], "float32"),
+    "ys": ("sbuf", [128, COLS], "float32"),
+    "one": ("sbuf", [128, TERMS * 128], "bfloat16"),
+    "ps": ("psum", [128, 512 * MAPS], "float32"),
+}
+SEMAPHORES = ["v", "s", "t", "dx", "dl", "dw0", "dw1", "dm", "dy", "near", "far", "gone"]
+
+
+def rank_program(g, core, T, topo):
+    r = T.rank_of(core)
+    if r is None:
+        return
+    cores = list(T.cores)
+
+    def near_of(d):
+        return [s for s in range(N) if s != d and cores[s] in topo.cores_of(cores[d])]
+
+    def far_of(d):
+        return [s for s in range(N) if cores[s] not in topo.cores_of(cores[d])]
+
+    near, far = near_of(r)[0], far_of(r)
+    Copy, add = ActivationFunctionType.Copy, AluOpType.add
+
+    queue = {"v": g.vector, "s": g.scalar, "t": g.tensor, "y": g.sync, "g": g}
+    count, seen = {}, {}
+
+    def wait(q, deps):
+        for sem, n in deps:
+            if seen.get((q, sem), 0) < n:
+                queue[q].wait_ge(T.sem[sem], n)
+                seen[(q, sem)] = n
+
+    def run(q, deps, call, sem=None, n=1):
+        wait(q, deps)
+        sem = sem or q
+        call(queue[q]).then_inc(T.sem[sem], n)
+        count[sem] = count.get(sem, 0) + n
+        return (sem, count[sem])
+
+    run("y", [], lambda q: q.dma_start(T.xs[0:32, :], T.x[0:32, :]), "dx", 16)
+    run("s", [], lambda q: q.dma_start(T.sl[0:16, :], T.send[:]), "dl", 16)
+    lx = run("y", [], lambda q: q.dma_start(T.xs[32:128, :], T.x[32:128, :]), "dx", 16)
+    ll = run("s", [], lambda q: q.dma_start(T.sl[16:32, :], T.send[:]), "dl", 16)
+    lw = []
+    for i in range(2):
+        a, b = 2048 * i, 2048 * i + 2048
+        lw.append(run("s", [], lambda q: q.dma_start(T.wt[:, a:b], T.w[:, a:b]), "dw%d" % i, 16))
+    for i in range(8):
+        lm = run("y", [lx], lambda q: q.dma_start(T.ml[16 * i:16 * i + 16, :], T.mp[:]), "dm", 16)
+
+    m3 = run("v", [], lambda q: q.memset(T.win[:, 0:MAPS * WIN:WIN], 0.0))
+    n1 = TERMS * max(b - a for j, (a, b) in enumerate(CUT) if len(SM[j]) == TERMS)
+    one = run("v", [], lambda q: q.memset(T.one[:, 0:n1], 1.0))
+    one = run("v", [one], lambda q: q.memset(T.one[:, 0:n1:TERMS], 0.0))
+
+    c = CAPP // 16
+    for p in range(0, 128, 32):
+        so = run("v", [ll], lambda q: q.tensor_scalar(T.so[p:p + 32, :], T.sl[0:32, :], 0.0, 4.0,
+                                                      AluOpType.max, AluOpType.mult))
+
+    def gather(to, d, n, qs):
+        last = {}
+        for t, q in enumerate(qs):
+            o = T.h[:, 4 * to + t:4 * (to + CAPP * n):4]
+            i = T.xs[:, t:4 * COLS].indirect(T.so[:, c * d:c * (d + n)])
+            if q == "v":
+                last[q] = run("v", [so, lx], lambda e: e.tensor_copy(o, i))
+            else:
+                last[q] = run("s", [so, lx], lambda e: e.activation(o, i, Copy))
+        return list(last.values())
+
+    used = []
+
+    def address(d, n):
+        e = [e for e in topo.engines(core, cores[d]) if e not in used][:n]
+        used.extend(e)
+        rid, pid = topo.addr(cores[d], core)
+        return {"dst_ids": [DstId(rid=rid, pnc=pid)], "dma_engine_mask": sum(1 << x for x in e),
+                "remote_sem": T.sem.near if d == near else T.sem.far}
+
+    def place(d):
+        return COLS + CAPP * [s for s in range(N) if s != d].index(r)
+
+    def send(ranks, to, q, s, first):
+        for src, dst, codes in ((q, T.qf, True), (s, T.sf, False)):
+            out = []
+            for i, d in enumerate(ranks):
+                a, b = first + CAPP * i, place(d)
+                a, b = src[:, a:a + CAPP], dst[:, b:b + CAPP]
+                if codes:
+                    a, b = a.bitcast(dt.uint8), b.bitcast(dt.uint8)
+                out.append(RemoteDMATransfer(srcs=[a], dsts=[b], **to[i]))
+            g.remote_dma_fused(out, local_sem=T.sem.gone)
+
+    to = [address(d, 4) for d in far]
+    hf = gather(0, far[0], 2, "vsvs")
+    qh = run("v", hf, lambda q: q.quantize_mx(T.hq[:], T.hs[:], T.h[:, 0:8 * CAPP]))
+    wait("g", [qh])
+    send(far, to, T.hq, T.hs, 0)
+    hn = gather(2 * CAPP, near, 1, "ssss")
+
+    qx = run("v", [lx], lambda q: q.quantize_mx(T.qf[:, 0:COLS], T.sf[:, 0:COLS], T.xs[:]))
+    qw = []
+    for i in range(4):
+        if i == 2:
+            qh = run("v", hf + hn, lambda q: q.quantize_mx(T.nq[:], T.ns[:], T.h[:, 4 * (SLOTS - 128):4 * SLOTS]))
+            wait("g", [qh])
+            send([near], [address(near, NE)], T.nq, T.ns, 128 - CAPP)
+            wait("g", [("gone", 2 * len(used))])
+        a, b = 256 * i, 256 * i + 256
+        qw.append(run("v", [lw[i // 2]], lambda q: q.quantize_mx(T.qw[:, a:b], T.sw[:, a:b], T.wt[:, 4 * a:4 * b])))
+    arrived = [("near", 2 * NE), ("far", 2 * 8)]
+
+    def product(k, a, b, deps):
+        return run("t", [qw[k // 2]] + deps, lambda q: q.matmul_mx(
+            T.ps[:, 512 * k:512 * k + b - a], T.qw[:, 128 * k:128 * k + 128], T.sw[:, 128 * k:128 * k + 128],
+            T.qf[:, a:b], T.sf[:, a:b], True, True))
+
+    def keep(q, k, n, to, dep):
+        o, i = T.win[:, k * WIN + to:k * WIN + to + n], T.ps[:, 512 * k:512 * k + n]
+        if q == "v":
+            return run("v", [dep], lambda e: e.tensor_copy(o, i))
+        return run("s", [dep], lambda e: e.activation(o, i, Copy))
+
+    own = [product(k, 0, COLS, [qx]) for k in range(MAPS)]
+    mt = run("v", [lm], lambda q: q.tensor_scalar(T.mt[:], T.ml[:], float(COLS + CAPP * (r + 1)), float(-CAPP),
+                                                  AluOpType.is_ge, AluOpType.mult))
+    mu = run("v", [mt, lm], lambda q: q.tensor_tensor(T.mu[:], T.ml[:], T.mt[:], add))
+    mo = run("v", [mu], lambda q: q.tensor_scalar(T.mo[:], T.mu[:], 1.0, None, add))
+    ev = [keep("v" if k in VOWN else "s", k, COLS, 1, own[k]) for k in range(MAPS)]
+    fr = [product(k, COLS, COLS + SLOTS, [ev[k]] + arrived) for k in range(MAPS)]
+    done, got = {}, {}
+    base = [m3, mo]
+
+    def evac(q, k):
+        done[k] = [ev[k], keep(q, k, SLOTS, 1 + COLS, fr[k])]
+
+    def pick(k, j):
+        a, b = CUT[j]
+        return T.win[:, k * WIN:k * WIN + WIN].indirect(T.mo[:, 32 * k + a // 16:32 * k + b // 16])
+
+    def spot(i, j):
+        a, b = CUT[j]
+        return T.pq[:, TERMS * a + i:TERMS * b:TERMS]
+
+    def side(buf, i, j):
+        a, b = CUT[j]
+        return buf[:, COLS * i + a:COLS * i + b]
+
+    def spick(k, j):
+        i = SM[j].index(k)
+        o = side(T.gs, 0, j) if i == 0 else spot(i, j)
+        got[k, j] = run("s", base + done[k], lambda q: q.activation(o, pick(k, j), Copy))
+
+    def vpick(k, j):
+        i = VM[j].index(k)
+        if i == 0:
+            dep, more = got[SM[j][0], j], side(T.gs, 0, j)
+        else:
+            dep, more = got[VM[j][i - 1], j], side(T.vs, i - 1, j)
+        o = spot(i, j) if len(SM[j]) == TERMS else side(T.vs, i, j)
+        got[k, j] = run("v", base + done[k] + [dep], lambda q: q.tensor_tensor(o, pick(k, j), more, add))
+
+    def scan(j):
+        a, b = TERMS * CUT[j][0], TERMS * CUT[j][1]
+        got["z", j] = run("v", [one] + [got[k, j] for k in range(MAPS) if k != VM[j][-1]], lambda q: q.tensor_tensor_scan(
+            T.zz[:, a:b], T.one[:, 0:b - a], T.pq[:, a:b], 0.0, AluOpType.mult, add))
+
+    def finish(j):
+        k, (a, b) = VM[j][-1], CUT[j]
+        if len(SM[j]) == TERMS:
+            dep, more = got["z", j], T.zz[:, TERMS * a + TERMS - 1:TERMS * b:TERMS]
+        else:
+            dep, more = got[VM[j][-2], j], side(T.vs, len(VM[j]) - 2, j)
+        v = run("v", base + done[k] + [dep], lambda q: q.tensor_tensor(T.ys[:, a:b], pick(k, j), more, add))
+        got["y"] = run("y", [v], lambda q: q.dma_start(T.y[:, a:b], T.ys[:, a:b]), "dy", 16)
+
+    def call(q, x):
+        if x[0] == "E":
+            return evac, (q, x[1]), []
+        j = x[-1]
+        before = [("P", k, j) for k in range(MAPS) if k != VM[j][-1]]
+        if x[0] == "Z":
+            return scan, (j,), before
+        if x[0] == "F":
+            return finish, (j,), [("E", VM[j][-1])] + ([("Z", j)] if len(SM[j]) == TERMS else before)
+        if q == "s":
+            return spick, (x[1], j), [("E", x[1])]
+        return vpick, (x[1], j), [("E", x[1])] + ([("P", SM[j][0], j)] if VM[j][0] == x[1] else [])
+
+    todo, have = {"s": list(ORDER["s"]), "v": list(ORDER["v"])}, set()
+    while todo["s"] or todo["v"]:
+        for q in "sv":
+            while todo[q]:
+                f, args, deps = call(q, todo[q][0])
+                if not all(x in have for x in deps):
+                    break
+                f(*args)
+                have.add(todo[q].pop(0))
+    wait("y", [got["y"]])

@@ -3,48 +3,47 @@ from concourse.mybir import dt, AluOpType, ActivationFunctionType
 
 COLS, MAPS, CAPP, N = 512, 8, 96, 4
 SLOTS = (N - 1) * CAPP
-WIN = 1 + COLS + SLOTS
+WIN = 1 + COLS + N * CAPP
 NE = 8
-CUT = [(0, 128), (128, 448), (448, 512)]
-VM = [[2, 7], [1, 2, 3, 4, 6, 5, 7], [5, 7]]
+PARTS = [(0, 1), (1, 2), (2, 4), (4, 8)]
+CUT = [(0, 160), (160, 352), (352, 448), (448, 512)]
+SCANNED = [2, 3]
+TERMS = 7
+FILLED = 3
 ORDER = {
-    "v": [("E", 0), ("E", 1), ("E", 2), ("P", 1, 1), ("P", 2, 1), ("P", 2, 0), ("P", 3, 1), ("P", 4, 1), ("P", 5, 2), ("P", 6, 1),
-          ("P", 5, 1), ("Z", 0), ("F", 1), ("Z", 2), ("F", 0), ("F", 2)],
-    "s": [("P", 0, 1), ("P", 1, 0), ("E", 3), ("E", 4), ("E", 5), ("E", 6), ("P", 0, 2), ("P", 6, 2), ("P", 4, 0), ("P", 5, 0),
-          ("P", 6, 0), ("P", 3, 0), ("P", 0, 0), ("P", 4, 2), ("P", 1, 2), ("P", 2, 2), ("E", 7), ("P", 3, 2)],
+    "v": [("G", 0, 0), ("G", 0, 2), ("Q", 0), ("G", 1, 0), ("X",), ("Q", 1), ("W", 0), ("W", 1), ("Q", 2), ("W", 2), ("W", 3)]
+    + [("O", k) for k in (2, 4, 6, 7)] + [("E", 1), ("E", 2)]
+    + [("P", k, j) for k in range(1, 7) for j in (0, 1)] + [("Z", 2), ("F", 7, 0, 1), ("Z", 3), ("F", 7, 2, 3)],
+    "s": [("G", 0, 1), ("G", 0, 3)] + [("G", 1, t) for t in (1, 2, 3)] + [("G", 2, t) for t in range(4)]
+    + [("O", k) for k in (0, 1, 3, 5)] + [("N", k) for k in (0, 1, 2)]
+    + [("E", 0), ("P", 0, 0), ("P", 0, 1), ("E", 3), ("P", 0, 2, 3), ("E", 4), ("E", 5), ("E", 6), ("P", 1, 2, 3), ("P", 2, 2, 3)]
+    + [("P", k, 2) for k in range(3, 7)] + [("E", 7)] + [("P", k, 3) for k in range(3, 7)],
 }
-SM = [[x[1] for x in ORDER["s"] if x[0] == "P" and x[2] == j] for j in range(len(CUT))]
-VOWN = [2, 5]
-TERMS = 6
 
 SCRATCH = {
     "xs": ("sbuf", [128, 4 * COLS], "bfloat16"),
     "wt": ("sbuf", [128, 512 * MAPS], "bfloat16"),
     "sl": ("sbuf", [32, N * CAPP // 16], "int32"),
     "so": ("sbuf", [128, N * CAPP // 16], "uint16"),
-    "ml": ("sbuf", [128, MAPS * COLS // 16], "int32"),
-    "mt": ("sbuf", [128, MAPS * COLS // 16], "int32"),
-    "mu": ("sbuf", [128, MAPS * COLS // 16], "int32"),
+    "ml": ("sbuf", [16, MAPS * COLS // 16], "int32"),
     "mo": ("sbuf", [128, MAPS * COLS // 16], "uint16"),
-    "h": ("sbuf", [128, 4 * SLOTS], "bfloat16"),
-    "hq": ("sbuf", [128, 2 * CAPP], "float8_e4m3fn_x4"),
-    "hs": ("sbuf", [128, 2 * CAPP], "uint8"),
-    "nq": ("sbuf", [128, 128], "float8_e4m3fn_x4"),
-    "ns": ("sbuf", [128, 128], "uint8"),
+    "h": ("sbuf", [128, 4 * (128 - CAPP + SLOTS)], "bfloat16"),
+    "hq": ("sbuf", [128, (N - 1) * 128], "float8_e4m3fn_x4"),
+    "hs": ("sbuf", [128, (N - 1) * 128], "uint8"),
     "qf": ("sbuf", [128, COLS + SLOTS], "float8_e4m3fn_x4"),
     "sf": ("sbuf", [128, COLS + SLOTS], "uint8"),
     "qw": ("sbuf", [128, 128 * MAPS], "float8_e4m3fn_x4"),
     "sw": ("sbuf", [128, 128 * MAPS], "uint8"),
     "win": ("sbuf", [128, MAPS * WIN], "float32"),
-    "gs": ("sbuf", [128, 2 * COLS], "float32"),
+    "gs": ("sbuf", [128, COLS], "float32"),
     "vs": ("sbuf", [128, MAPS * COLS], "float32"),
-    "pq": ("sbuf", [128, TERMS * COLS], "float32"),
-    "zz": ("sbuf", [128, TERMS * COLS], "float32"),
+    "pq": ("sbuf", [128, MAPS * COLS], "float32"),
+    "zz": ("sbuf", [128, MAPS * COLS], "float32"),
     "ys": ("sbuf", [128, COLS], "float32"),
-    "one": ("sbuf", [128, TERMS * 128], "bfloat16"),
+    "one": ("sbuf", [128, MAPS * 256], "bfloat16"),
     "ps": ("psum", [128, 512 * MAPS], "float32"),
 }
-SEMAPHORES = ["v", "s", "t", "dx", "dl", "dw0", "dw1", "dm", "dy", "near", "far", "gone"]
+SEMAPHORES = ["v", "s", "t", "g", "dx", "dl", "dw0", "dw1", "dm", "dr", "dy", "near", "far", "gone"]
 
 
 def rank_program(g, core, T, topo):
@@ -53,17 +52,16 @@ def rank_program(g, core, T, topo):
         return
     cores = list(T.cores)
 
-    def near_of(d):
-        return [s for s in range(N) if s != d and cores[s] in topo.cores_of(cores[d])]
+    def sources(d):
+        return sorted((s for s in range(N) if s != d), key=lambda s: cores[s] not in topo.cores_of(cores[d]))
 
-    def far_of(d):
-        return [s for s in range(N) if cores[s] not in topo.cores_of(cores[d])]
-
-    near, far = near_of(r)[0], far_of(r)
+    near, far = sources(r)[0], sources(r)[1:]
+    dest = sorted(far, key=lambda d: topo.die(cores[d]) == topo.die(core)) + [near]
     Copy, add = ActivationFunctionType.Copy, AluOpType.add
+    pad, c = 128 - CAPP, CAPP // 16
 
     queue = {"v": g.vector, "s": g.scalar, "t": g.tensor, "y": g.sync, "g": g}
-    count, seen = {}, {}
+    count, seen, got = {}, {}, {}
 
     def wait(q, deps):
         for sem, n in deps:
@@ -78,164 +76,180 @@ def rank_program(g, core, T, topo):
         count[sem] = count.get(sem, 0) + n
         return (sem, count[sem])
 
+    def copy(q, deps, o, i):
+        if q == "v":
+            return run("v", deps, lambda e: e.tensor_copy(o, i))
+        return run("s", deps, lambda e: e.activation(o, i, Copy))
+
+    lm = run("s", [], lambda q: q.dma_start(T.ml[:], T.mp[:]), "dm", 16)
     run("y", [], lambda q: q.dma_start(T.xs[0:32, :], T.x[0:32, :]), "dx", 16)
-    run("s", [], lambda q: q.dma_start(T.sl[0:16, :], T.send[:]), "dl", 16)
+    for q, p in (("s", 0), ("y", 16)):
+        ll = run(q, [], lambda e: e.dma_start(T.sl[p:p + 16, :], T.send[:]), "dl", 16)
     lx = run("y", [], lambda q: q.dma_start(T.xs[32:128, :], T.x[32:128, :]), "dx", 16)
-    ll = run("s", [], lambda q: q.dma_start(T.sl[16:32, :], T.send[:]), "dl", 16)
-    lw = []
-    for i in range(2):
-        a, b = 2048 * i, 2048 * i + 2048
-        lw.append(run("s", [], lambda q: q.dma_start(T.wt[:, a:b], T.w[:, a:b]), "dw%d" % i, 16))
-    for i in range(8):
-        lm = run("y", [lx], lambda q: q.dma_start(T.ml[16 * i:16 * i + 16, :], T.mp[:]), "dm", 16)
+    lw = [run("y", [], lambda q: q.dma_start(T.wt[:, a:a + 2048], T.w[:, a:a + 2048]), "dw%d" % (a // 2048), 16) for a in (0, 2048)]
 
-    m3 = run("v", [], lambda q: q.memset(T.win[:, 0:MAPS * WIN:WIN], 0.0))
-    n1 = TERMS * max(b - a for j, (a, b) in enumerate(CUT) if len(SM[j]) == TERMS)
-    one = run("v", [], lambda q: q.memset(T.one[:, 0:n1], 1.0))
-    one = run("v", [one], lambda q: q.memset(T.one[:, 0:n1:TERMS], 0.0))
-
-    c = CAPP // 16
+    h0 = run("v", [], lambda q: q.memset(T.h[:, 0:4 * pad], 0.0))
+    base = [run("v", [], lambda q: q.memset(T.win[:, 0:MAPS * WIN:WIN], 0.0))]
+    for k in range(MAPS):
+        a = k * WIN + 1 + COLS + CAPP * r
+        if k < FILLED:
+            base.append(run("g", [], lambda q: q.iota(T.win[:, a:a + CAPP], [[0, CAPP]], 0, 0, allow_small_or_imprecise_dtypes=True)))
+        else:
+            base.append(copy("s", [h0], T.win[:, a:a + CAPP], T.h[:, 0:CAPP]))
+    n = TERMS * max(CUT[j][1] - CUT[j][0] for j in SCANNED)
+    one = run("v", [], lambda q: q.memset(T.one[:, 0:n], 1.0))
+    one = run("v", [one], lambda q: q.memset(T.one[:, 0:n:TERMS], 0.0))
+    mo = run("v", [lm], lambda q: q.tensor_scalar(T.mo[0:16, :], T.ml[:], 1.0, None, add))
+    for p in range(16, 128, 16):
+        mr = run("y", [mo], lambda q: q.dma_start(T.mo[p:p + 16, :], T.mo[0:16, :]), "dr", 16)
+    base += [mo, mr]
     for p in range(0, 128, 32):
-        so = run("v", [ll], lambda q: q.tensor_scalar(T.so[p:p + 32, :], T.sl[0:32, :], 0.0, 4.0,
-                                                      AluOpType.max, AluOpType.mult))
+        so = run("v", [ll], lambda q: q.tensor_scalar(T.so[p:p + 32, :], T.sl[:], 0.0, 4.0, AluOpType.max, AluOpType.mult))
 
-    def gather(to, d, n, qs):
-        last = {}
-        for t, q in enumerate(qs):
-            o = T.h[:, 4 * to + t:4 * (to + CAPP * n):4]
-            i = T.xs[:, t:4 * COLS].indirect(T.so[:, c * d:c * (d + n)])
-            if q == "v":
-                last[q] = run("v", [so, lx], lambda e: e.tensor_copy(o, i))
+    off = topo.engines(core, cores[far[0]])[:NE]
+    on = [e for e in topo.engines(core, cores[near]) if e not in off][:NE]
+
+    def send(pairs, codes):
+        out = []
+        for i, e in pairs:
+            d = dest[i]
+            rid, pid = topo.addr(cores[d], core)
+            a, b = 128 * i + pad, COLS + CAPP * sources(d).index(r)
+            if codes:
+                a, b = T.hq[:, a:a + CAPP].bitcast(dt.uint8), T.qf[:, b:b + CAPP].bitcast(dt.uint8)
             else:
-                last[q] = run("s", [so, lx], lambda e: e.activation(o, i, Copy))
-        return list(last.values())
+                a, b = T.hs[:, a:a + CAPP], T.sf[:, b:b + CAPP]
+            out.append(RemoteDMATransfer(srcs=[a], dsts=[b], dst_ids=[DstId(rid=rid, pnc=pid)], dma_engine_mask=sum(1 << x for x in e),
+                                         remote_sem=T.sem.near if d == near else T.sem.far))
+            count["gone"] = count.get("gone", 0) + len(e)
+        g.remote_dma_fused(out, local_sem=T.sem.gone)
 
-    used = []
+    here, there = ("near", 2 * len(on)), ("far", 3 * len(off))
 
-    def address(d, n):
-        e = [e for e in topo.engines(core, cores[d]) if e not in used][:n]
-        used.extend(e)
-        rid, pid = topo.addr(cores[d], core)
-        return {"dst_ids": [DstId(rid=rid, pnc=pid)], "dma_engine_mask": sum(1 << x for x in e),
-                "remote_sem": T.sem.near if d == near else T.sem.far}
+    def gather(q, i, t):
+        a, b = 4 * (pad + CAPP * i), c * dest[i]
+        return copy(q, [so, lx], T.h[:, a + t:a + 4 * CAPP:4], T.xs[:, t:4 * COLS].indirect(T.so[:, b:b + c]))
 
-    def place(d):
-        return COLS + CAPP * [s for s in range(N) if s != d].index(r)
-
-    def send(ranks, to, q, s, first):
-        for src, dst, codes in ((q, T.qf, True), (s, T.sf, False)):
-            out = []
-            for i, d in enumerate(ranks):
-                a, b = first + CAPP * i, place(d)
-                a, b = src[:, a:a + CAPP], dst[:, b:b + CAPP]
-                if codes:
-                    a, b = a.bitcast(dt.uint8), b.bitcast(dt.uint8)
-                out.append(RemoteDMATransfer(srcs=[a], dsts=[b], **to[i]))
-            g.remote_dma_fused(out, local_sem=T.sem.gone)
-
-    to = [address(d, 4) for d in far]
-    hf = gather(0, far[0], 2, "vsvs")
-    qh = run("v", hf, lambda q: q.quantize_mx(T.hq[:], T.hs[:], T.h[:, 0:8 * CAPP]))
-    wait("g", [qh])
-    send(far, to, T.hq, T.hs, 0)
-    hn = gather(2 * CAPP, near, 1, "ssss")
-
-    qx = run("v", [lx], lambda q: q.quantize_mx(T.qf[:, 0:COLS], T.sf[:, 0:COLS], T.xs[:]))
-    qw = []
-    for i in range(4):
-        if i == 2:
-            qh = run("v", hf + hn, lambda q: q.quantize_mx(T.nq[:], T.ns[:], T.h[:, 4 * (SLOTS - 128):4 * SLOTS]))
-            wait("g", [qh])
-            send([near], [address(near, NE)], T.nq, T.ns, 128 - CAPP)
-            wait("g", [("gone", 2 * len(used))])
-        a, b = 256 * i, 256 * i + 256
-        qw.append(run("v", [lw[i // 2]], lambda q: q.quantize_mx(T.qw[:, a:b], T.sw[:, a:b], T.wt[:, 4 * a:4 * b])))
-    arrived = [("near", 2 * NE), ("far", 2 * 8)]
+    def pack(q, i):
+        v = run(q, [h0] + [got["G", x, t] for x in range(i + 1) for t in range(4)], lambda e: e.quantize_mx(
+            T.hq[:, 128 * i:128 * i + 128], T.hs[:, 128 * i:128 * i + 128], T.h[:, 4 * CAPP * i:4 * (CAPP * i + 128)]))
+        wait("g", [v])
+        if dest[i] != near:
+            send([(i, off)], True)
+        else:
+            send([(0, off[:NE // 2]), (1, off[NE // 2:]), (i, on)], False)
+            send([(i, on)], True)
+            wait("g", [("gone", count["gone"])])
+        return v
 
     def product(k, a, b, deps):
-        return run("t", [qw[k // 2]] + deps, lambda q: q.matmul_mx(
+        return run("t", deps, lambda q: q.matmul_mx(
             T.ps[:, 512 * k:512 * k + b - a], T.qw[:, 128 * k:128 * k + 128], T.sw[:, 128 * k:128 * k + 128],
             T.qf[:, a:b], T.sf[:, a:b], True, True))
 
-    def keep(q, k, n, to, dep):
-        o, i = T.win[:, k * WIN + to:k * WIN + to + n], T.ps[:, 512 * k:512 * k + n]
-        if q == "v":
-            return run("v", [dep], lambda e: e.tensor_copy(o, i))
-        return run("s", [dep], lambda e: e.activation(o, i, Copy))
+    def own(q):
+        return run(q, [lx], lambda e: e.quantize_mx(T.qf[:, 0:COLS], T.sf[:, 0:COLS], T.xs[:]))
 
-    own = [product(k, 0, COLS, [qx]) for k in range(MAPS)]
-    mt = run("v", [lm], lambda q: q.tensor_scalar(T.mt[:], T.ml[:], float(COLS + CAPP * (r + 1)), float(-CAPP),
-                                                  AluOpType.is_ge, AluOpType.mult))
-    mu = run("v", [mt, lm], lambda q: q.tensor_tensor(T.mu[:], T.ml[:], T.mt[:], add))
-    mo = run("v", [mu], lambda q: q.tensor_scalar(T.mo[:], T.mu[:], 1.0, None, add))
-    ev = [keep("v" if k in VOWN else "s", k, COLS, 1, own[k]) for k in range(MAPS)]
-    fr = [product(k, COLS, COLS + SLOTS, [ev[k]] + arrived) for k in range(MAPS)]
-    done, got = {}, {}
-    base = [m3, mo]
+    def maps(q, i):
+        a, b = 128 * PARTS[i][0], 128 * PARTS[i][1]
+        v = run(q, [lw[PARTS[i][0] // 4]], lambda e: e.quantize_mx(T.qw[:, a:b], T.sw[:, a:b], T.wt[:, 4 * a:4 * b]))
+        for k in range(*PARTS[i]):
+            got["M", k] = product(k, 0, COLS, [v, got["X",]])
+        return v
 
-    def evac(q, k):
-        done[k] = [ev[k], keep(q, k, SLOTS, 1 + COLS, fr[k])]
+    def keep(q, dep, k, a, n, to):
+        return copy(q, [dep], T.win[:, k * WIN + to:k * WIN + to + n], T.ps[:, 512 * k + a:512 * k + a + n])
 
-    def pick(k, j):
-        a, b = CUT[j]
+    early = [x[1] for q in "vs" for x in ORDER[q] if x[0] == "N"]
+
+    def keep_own(q, k):
+        return keep(q, got["M", k], k, 0, COLS, 1)
+
+    def keep_near(q, k):
+        for x in [x for x in early if x <= k and ("B", x) not in got]:
+            got["B", x] = product(x, COLS - pad, COLS + CAPP, [got["O", x], here])
+        return keep(q, got["B", k], k, pad, CAPP, 1 + COLS + CAPP * near)
+
+    def keep_far(q, k):
+        for x in [x for x in range(k + 1) if ("A", x) not in got]:
+            got["A", x] = product(x, COLS + CAPP * (x in early), COLS + SLOTS, [got["N" if x in early else "O", x], here, there])
+        if k in early:
+            return keep(q, got["A", k], k, 0, 2 * CAPP, 1 + COLS + CAPP * far[0])
+        if near + 1 == far[0]:
+            return keep(q, got["A", k], k, 0, SLOTS, 1 + COLS + CAPP * near)
+        keep(q, got["A", k], k, 0, CAPP, 1 + COLS + CAPP * near)
+        return keep(q, got["A", k], k, CAPP, 2 * CAPP, 1 + COLS + CAPP * far[0])
+
+    def terms(q, j):
+        return [x[1] for x in ORDER[q] if x[0] == "P" and x[2] <= j <= x[-1]]
+
+    def pick(k, a, b):
         return T.win[:, k * WIN:k * WIN + WIN].indirect(T.mo[:, 32 * k + a // 16:32 * k + b // 16])
 
-    def spot(i, j):
-        a, b = CUT[j]
+    def ready(k):
+        return base + [got["O", k], got["E", k]] + ([got["N", k]] if k in early else [])
+
+    def spot(i, a, b):
         return T.pq[:, TERMS * a + i:TERMS * b:TERMS]
 
-    def side(buf, i, j):
-        a, b = CUT[j]
-        return buf[:, COLS * i + a:COLS * i + b]
-
-    def spick(k, j):
-        i = SM[j].index(k)
-        o = side(T.gs, 0, j) if i == 0 else spot(i, j)
-        got[k, j] = run("s", base + done[k], lambda q: q.activation(o, pick(k, j), Copy))
-
-    def vpick(k, j):
-        i = VM[j].index(k)
+    def before(k, j, a=0, b=16):
+        mine = terms("v", j)
+        i = mine.index(k) if k in mine else len(mine)
+        if k not in mine and j in SCANNED:
+            return ("Z", j), T.zz[:, TERMS * a + TERMS - 1:TERMS * b:TERMS]
         if i == 0:
-            dep, more = got[SM[j][0], j], side(T.gs, 0, j)
-        else:
-            dep, more = got[VM[j][i - 1], j], side(T.vs, i - 1, j)
-        o = spot(i, j) if len(SM[j]) == TERMS else side(T.vs, i, j)
-        got[k, j] = run("v", base + done[k] + [dep], lambda q: q.tensor_tensor(o, pick(k, j), more, add))
+            return ("P", terms("s", j)[0], j), T.gs[:, a:b]
+        return ("P", mine[i - 1], j), T.vs[:, COLS * (i - 1) + a:COLS * (i - 1) + b]
 
-    def scan(j):
+    def term(q, k, j, last=None):
+        js = range(j, (last or j) + 1)
+        a, b = CUT[j][0], CUT[js[-1]][1]
+        mine = terms(q, j)
+        i = mine.index(k)
+        assert all(terms(q, x).index(k) == i for x in js)
+        if q == "s":
+            v = copy(q, ready(k), T.gs[:, a:b] if i == 0 and terms("v", j) else spot(i, a, b), pick(k, a, b))
+        else:
+            o = spot(0, a, b) if j in SCANNED and i == len(mine) - 1 else T.vs[:, COLS * i + a:COLS * i + b]
+            v = run(q, ready(k) + [got[before(k, x)[0]] for x in js], lambda e: e.tensor_tensor(o, pick(k, a, b), before(k, j, a, b)[1], add))
+        got.update({("P", k, x): v for x in js})
+        return v
+
+    def scan(q, j):
         a, b = TERMS * CUT[j][0], TERMS * CUT[j][1]
-        got["z", j] = run("v", [one] + [got[k, j] for k in range(MAPS) if k != VM[j][-1]], lambda q: q.tensor_tensor_scan(
+        return run(q, [one] + [got["P", k, j] for k in terms("v", j) + terms("s", j)], lambda e: e.tensor_tensor_scan(
             T.zz[:, a:b], T.one[:, 0:b - a], T.pq[:, a:b], 0.0, AluOpType.mult, add))
 
-    def finish(j):
-        k, (a, b) = VM[j][-1], CUT[j]
-        if len(SM[j]) == TERMS:
-            dep, more = got["z", j], T.zz[:, TERMS * a + TERMS - 1:TERMS * b:TERMS]
-        else:
-            dep, more = got[VM[j][-2], j], side(T.vs, len(VM[j]) - 2, j)
-        v = run("v", base + done[k] + [dep], lambda q: q.tensor_tensor(T.ys[:, a:b], pick(k, j), more, add))
-        got["y"] = run("y", [v], lambda q: q.dma_start(T.y[:, a:b], T.ys[:, a:b]), "dy", 16)
+    def finish(q, k, j, last=None):
+        js = range(j, (last or j) + 1)
+        a, b = CUT[j][0], CUT[js[-1]][1]
+        v = run(q, ready(k) + [got[before(k, x)[0]] for x in js], lambda e: e.tensor_tensor(
+            T.ys[:, a:b], pick(k, a, b), before(k, j, a, b)[1], add))
+        got["y"] = run("y", [v], lambda e: e.dma_start(T.y[:, a:b], T.ys[:, a:b]), "dy", 16)
+        return v
 
-    def call(q, x):
+    def needs(q, x):
+        if x[0] == "Q":
+            return [("G", i, t) for i in range(x[1] + 1) for t in range(4)]
+        if x[0] == "O":
+            return [("W", i) for i, (a, b) in enumerate(PARTS) if a <= x[1] < b]
+        if x[0] == "N":
+            return [("W", len(PARTS) - 1)] + [("O", k) for k in early if k <= x[1]]
         if x[0] == "E":
-            return evac, (q, x[1]), []
-        j = x[-1]
-        before = [("P", k, j) for k in range(MAPS) if k != VM[j][-1]]
+            return [("O", k) for k in range(x[1] + 1)] + [("N", k) for k in early]
         if x[0] == "Z":
-            return scan, (j,), before
-        if x[0] == "F":
-            return finish, (j,), [("E", VM[j][-1])] + ([("Z", j)] if len(SM[j]) == TERMS else before)
-        if q == "s":
-            return spick, (x[1], j), [("E", x[1])]
-        return vpick, (x[1], j), [("E", x[1])] + ([("P", SM[j][0], j)] if VM[j][0] == x[1] else [])
+            return [("P", k, x[1]) for k in terms("v", x[1]) + terms("s", x[1])]
+        if x[0] in "PF":
+            return [("E", x[1])] + ([before(x[1], j)[0] for j in range(x[2], x[-1] + 1)] if q == "v" else [])
+        return []
 
-    todo, have = {"s": list(ORDER["s"]), "v": list(ORDER["v"])}, set()
+    calls = {"G": gather, "Q": pack, "X": own, "W": maps, "O": keep_own, "N": keep_near, "E": keep_far, "P": term, "Z": scan, "F": finish}
+    todo = {q: list(ORDER[q]) for q in "sv"}
     while todo["s"] or todo["v"]:
+        left = len(todo["s"]) + len(todo["v"])
         for q in "sv":
-            while todo[q]:
-                f, args, deps = call(q, todo[q][0])
-                if not all(x in have for x in deps):
-                    break
-                f(*args)
-                have.add(todo[q].pop(0))
+            while todo[q] and all(x in got for x in needs(q, todo[q][0])):
+                x = todo[q].pop(0)
+                got[x] = calls[x[0]](q, *x[1:])
+        assert len(todo["s"]) + len(todo["v"]) < left
     wait("y", [got["y"]])

@@ -4,20 +4,27 @@ from concourse.mybir import dt, AluOpType, ActivationFunctionType
 COLS, MAPS, CAPP, N = 512, 8, 96, 4
 SLOTS = (N - 1) * CAPP
 WIN = 1 + COLS + N * CAPP
-NE = 8
-PARTS = [(0, 1), (1, 2), (2, 4), (4, 8)]
-CUT = [(0, 160), (160, 352), (352, 448), (448, 512)]
+PARTS = [(0, 1), (1, 2), (2, 4), (4, 6), (6, 8)]
+BATCH = [(0, 96), (96, 192), (192, 288)]
+SENDS = [[(True, [(0, 0, 96)]), (False, [(0, 0, 96)])], [(True, [(1, 96, 192)])], [(True, [(2, 192, 288)]), (False, [(1, 96, 192), (2, 192, 288)])]]
+CUT = [(0, 192), (192, 352), (352, 448), (448, 512)]
+STAGES = [2]
+HELD = [2]
+BANK = {(0, 0, 2): 3, (1, 0, 2): 4}
 SCANNED = [2, 3]
 TERMS = 7
-FILLED = 3
+FILLED = 1
 ORDER = {
-    "v": [("G", 0, 0), ("G", 0, 2), ("Q", 0), ("G", 1, 0), ("X",), ("Q", 1), ("W", 0), ("W", 1), ("Q", 2), ("W", 2), ("W", 3)]
-    + [("O", k) for k in (2, 4, 6, 7)] + [("E", 1), ("E", 2)]
-    + [("P", k, j) for k in range(1, 7) for j in (0, 1)] + [("Z", 2), ("F", 7, 0, 1), ("Z", 3), ("F", 7, 2, 3)],
-    "s": [("G", 0, 1), ("G", 0, 3)] + [("G", 1, t) for t in (1, 2, 3)] + [("G", 2, t) for t in range(4)]
-    + [("O", k) for k in (0, 1, 3, 5)] + [("N", k) for k in (0, 1, 2)]
-    + [("E", 0), ("P", 0, 0), ("P", 0, 1), ("E", 3), ("P", 0, 2, 3), ("E", 4), ("E", 5), ("E", 6), ("P", 1, 2, 3), ("P", 2, 2, 3)]
-    + [("P", k, 2) for k in range(3, 7)] + [("E", 7)] + [("P", k, 3) for k in range(3, 7)],
+    "v": [("G", 0, 0), ("G", 0, 2), ("G", 2, 0), ("Q", 0), ("X",), ("W", 0), ("W", 1), ("Q", 1), ("W", 2), ("Q", 2), ("W", 3), ("W", 4)]
+    + [("O", k) for k in (3, 5, 7)] + [("E", 0, 0, 2), ("E", 1, 0, 2), ("E", 1, 2, 3), ("E", 2, 0, 3)]
+    + [x for a, b in zip((1, 2, 3, 4, 5), (1, 3, 4, 5, 6)) for x in (("P", a, 1), ("P", b, 0))]
+    + [("P", 6, 1), ("F", 7, 0), ("F", 7, 1), ("Z", 2), ("Z", 3), ("F", 7, 2), ("F", 7, 3)],
+    "s": [("G", 0, 1), ("G", 0, 3)] + [("G", 1, t) for t in range(4)] + [("G", 2, t) for t in (1, 2, 3)]
+    + [("O", k) for k in (0, 1, 2, 4, 6)]
+    + [("E", 0, 2, 3), ("P", 0, 1), ("P", 0, 0), ("E", 3, 0, 3), ("E", 4, 0, 3), ("B", 2, 0), ("E", 5, 0, 3), ("E", 6, 0, 3)]
+    + [("P", 0, 2, 3), ("E", 7, 0, 3), ("P", 1, 2, 3)] + [("P", k, j) for j in (2, 3) for k in range(2, 7)],
+    "t": [("A", k) for k in (0, 1, 2, 3, 4, 5, 7, 6)] + [("A", k, a, b) for a, b in ((0, 2), (2, 3)) for k in (0, 1)]
+    + [("A", k, 0, 3) for k in range(2, MAPS)],
 }
 
 SCRATCH = {
@@ -27,23 +34,23 @@ SCRATCH = {
     "so": ("sbuf", [128, N * CAPP // 16], "uint16"),
     "ml": ("sbuf", [16, MAPS * COLS // 16], "int32"),
     "mo": ("sbuf", [128, MAPS * COLS // 16], "uint16"),
-    "h": ("sbuf", [128, 4 * (128 - CAPP + SLOTS)], "bfloat16"),
-    "hq": ("sbuf", [128, (N - 1) * 128], "float8_e4m3fn_x4"),
-    "hs": ("sbuf", [128, (N - 1) * 128], "uint8"),
+    "h": ("sbuf", [128, 4 * (128 + SLOTS)], "bfloat16"),
+    "hq": ("sbuf", [128, 128 * 6], "float8_e4m3fn_x4"),
+    "hs": ("sbuf", [128, 128 * 6], "uint8"),
     "qf": ("sbuf", [128, COLS + SLOTS], "float8_e4m3fn_x4"),
     "sf": ("sbuf", [128, COLS + SLOTS], "uint8"),
     "qw": ("sbuf", [128, 128 * MAPS], "float8_e4m3fn_x4"),
     "sw": ("sbuf", [128, 128 * MAPS], "uint8"),
     "win": ("sbuf", [128, MAPS * WIN], "float32"),
-    "gs": ("sbuf", [128, COLS], "float32"),
     "vs": ("sbuf", [128, MAPS * COLS], "float32"),
+    "bs": ("sbuf", [128, COLS], "float32"),
     "pq": ("sbuf", [128, MAPS * COLS], "float32"),
     "zz": ("sbuf", [128, MAPS * COLS], "float32"),
     "ys": ("sbuf", [128, COLS], "float32"),
     "one": ("sbuf", [128, MAPS * 256], "bfloat16"),
     "ps": ("psum", [128, 512 * MAPS], "float32"),
 }
-SEMAPHORES = ["v", "s", "t", "g", "dx", "dl", "dw0", "dw1", "dm", "dr", "dy", "near", "far", "gone"]
+SEMAPHORES = ["v", "s", "t", "dx", "dl", "dw0", "dw1", "dm", "dr", "dg", "db", "dy", "da", "in0", "in1", "in2", "gone"]
 
 
 def rank_program(g, core, T, topo):
@@ -52,13 +59,16 @@ def rank_program(g, core, T, topo):
         return
     cores = list(T.cores)
 
-    def sources(d):
-        return sorted((s for s in range(N) if s != d), key=lambda s: cores[s] not in topo.cores_of(cores[d]))
+    def dests(s):
+        others = [d for d in range(N) if d != s]
+        return sorted(others, key=lambda d: (cores[d] in topo.cores_of(cores[s]), topo.die(cores[d]) == topo.die(cores[s])))
 
-    near, far = sources(r)[0], sources(r)[1:]
-    dest = sorted(far, key=lambda d: topo.die(cores[d]) == topo.die(core)) + [near]
+    def sources(d):
+        return sorted((s for s in range(N) if s != d), key=lambda s: min((dests(s).index(d) + 1) % (N - 1), STAGES[0]))
+
+    dest, src = dests(r), sources(r)
     Copy, add = ActivationFunctionType.Copy, AluOpType.add
-    pad, c = 128 - CAPP, CAPP // 16
+    pad, c = max(CAPP // 4, 128 - BATCH[0][1]), CAPP // 16
 
     queue = {"v": g.vector, "s": g.scalar, "t": g.tensor, "y": g.sync, "g": g}
     count, seen, got = {}, {}, {}
@@ -81,19 +91,23 @@ def rank_program(g, core, T, topo):
             return run("v", deps, lambda e: e.tensor_copy(o, i))
         return run("s", deps, lambda e: e.activation(o, i, Copy))
 
+    split = [j for x in ORDER["s"] if x[0] == "B" for j in x[2:]]
+
     lm = run("s", [], lambda q: q.dma_start(T.ml[:], T.mp[:]), "dm", 16)
     run("y", [], lambda q: q.dma_start(T.xs[0:32, :], T.x[0:32, :]), "dx", 16)
     for q, p in (("s", 0), ("y", 16)):
         ll = run(q, [], lambda e: e.dma_start(T.sl[p:p + 16, :], T.send[:]), "dl", 16)
     lx = run("y", [], lambda q: q.dma_start(T.xs[32:128, :], T.x[32:128, :]), "dx", 16)
-    lw = [run("y", [], lambda q: q.dma_start(T.wt[:, a:a + 2048], T.w[:, a:a + 2048]), "dw%d" % (a // 2048), 16) for a in (0, 2048)]
+    lw = [run(q, [], lambda e: e.dma_start(T.wt[p:z, a:a + 2048], T.w[p:z, a:a + 2048]), sem, 16)
+          for q, sem, a, p, z in (("y", "dw0", 0, 0, 128), ("y", "dw1", 2048, 0, 112), ("g", "dg", 2048, 112, 128))]
+    lw = [lw[:1], lw[1:]]
 
     h0 = run("v", [], lambda q: q.memset(T.h[:, 0:4 * pad], 0.0))
     base = [run("v", [], lambda q: q.memset(T.win[:, 0:MAPS * WIN:WIN], 0.0))]
     for k in range(MAPS):
         a = k * WIN + 1 + COLS + CAPP * r
         if k < FILLED:
-            base.append(run("g", [], lambda q: q.iota(T.win[:, a:a + CAPP], [[0, CAPP]], 0, 0, allow_small_or_imprecise_dtypes=True)))
+            base.append(run("v", [], lambda q: q.memset(T.win[:, a:a + CAPP], 0.0)))
         else:
             base.append(copy("s", [h0], T.win[:, a:a + CAPP], T.h[:, 0:CAPP]))
     n = TERMS * max(CUT[j][1] - CUT[j][0] for j in SCANNED)
@@ -106,45 +120,48 @@ def rank_program(g, core, T, topo):
     for p in range(0, 128, 32):
         so = run("v", [ll], lambda q: q.tensor_scalar(T.so[p:p + 32, :], T.sl[:], 0.0, 4.0, AluOpType.max, AluOpType.mult))
 
-    off = topo.engines(core, cores[far[0]])[:NE]
-    on = [e for e in topo.engines(core, cores[near]) if e not in off][:NE]
+    off = topo.engines(core, cores[dest[0]])
+    on = [e for e in topo.engines(core, cores[dest[-1]]) if e not in off]
 
-    def send(pairs, codes):
+    def engines(x, which):
+        far = [y for y in which if y[1] // CAPP != N - 2]
+        return off[far.index(x)::len(far)] if x in far else on
+
+    landed = [("in%d" % u, sum(len(engines(x, w)) for y in SENDS for _, w in y for x in w if (x[1] // CAPP + 1) % (N - 1) == u))
+              for u in range(N - 1)]
+
+    def send(codes, which):
         out = []
-        for i, e in pairs:
-            d = dest[i]
-            rid, pid = topo.addr(cores[d], core)
-            a, b = 128 * i + pad, COLS + CAPP * sources(d).index(r)
+        for i, lo, hi in which:
+            u, e = lo // CAPP, engines((i, lo, hi), which)
+            rid, pid = topo.addr(cores[dest[u]], core)
+            a, b, n = 192 * (i + 1) - BATCH[i][1] + lo, COLS + CAPP * sources(dest[u]).index(r) + lo % CAPP, hi - lo
             if codes:
-                a, b = T.hq[:, a:a + CAPP].bitcast(dt.uint8), T.qf[:, b:b + CAPP].bitcast(dt.uint8)
+                a, b = T.hq[:, a:a + n].bitcast(dt.uint8), T.qf[:, b:b + n].bitcast(dt.uint8)
             else:
-                a, b = T.hs[:, a:a + CAPP], T.sf[:, b:b + CAPP]
+                a, b = T.hs[:, a:a + n], T.sf[:, b:b + n]
             out.append(RemoteDMATransfer(srcs=[a], dsts=[b], dst_ids=[DstId(rid=rid, pnc=pid)], dma_engine_mask=sum(1 << x for x in e),
-                                         remote_sem=T.sem.near if d == near else T.sem.far))
+                                         remote_sem=T.sem[landed[(u + 1) % (N - 1)][0]]))
             count["gone"] = count.get("gone", 0) + len(e)
         g.remote_dma_fused(out, local_sem=T.sem.gone)
 
-    here, there = ("near", 2 * len(on)), ("far", 3 * len(off))
-
     def gather(q, i, t):
-        a, b = 4 * (pad + CAPP * i), c * dest[i]
-        return copy(q, [so, lx], T.h[:, a + t:a + 4 * CAPP:4], T.xs[:, t:4 * COLS].indirect(T.so[:, b:b + c]))
+        a, b = BATCH[i]
+        z = CAPP * (dest[a // CAPP] - a // CAPP) * (b - a <= CAPP)
+        return copy(q, [so, lx], T.h[:, 4 * (pad + a) + t:4 * (pad + b):4], T.xs[:, t:4 * COLS].indirect(T.so[:, (a + z) // 16:(b + z) // 16]))
 
     def pack(q, i):
+        a, b, n = 192 * (i + 1), pad + BATCH[i][1], max(128, BATCH[i][1] - BATCH[i][0])
         v = run(q, [h0] + [got["G", x, t] for x in range(i + 1) for t in range(4)], lambda e: e.quantize_mx(
-            T.hq[:, 128 * i:128 * i + 128], T.hs[:, 128 * i:128 * i + 128], T.h[:, 4 * CAPP * i:4 * (CAPP * i + 128)]))
+            T.hq[:, a - n:a], T.hs[:, a - n:a], T.h[:, 4 * (b - n):4 * b]))
         wait("g", [v])
-        if dest[i] != near:
-            send([(i, off)], True)
-        else:
-            send([(0, off[:NE // 2]), (1, off[NE // 2:]), (i, on)], False)
-            send([(i, on)], True)
-            wait("g", [("gone", count["gone"])])
+        for x in SENDS[i]:
+            send(*x)
         return v
 
-    def product(k, a, b, deps):
+    def product(k, bank, a, b, deps):
         return run("t", deps, lambda q: q.matmul_mx(
-            T.ps[:, 512 * k:512 * k + b - a], T.qw[:, 128 * k:128 * k + 128], T.sw[:, 128 * k:128 * k + 128],
+            T.ps[:, 512 * bank:512 * bank + b - a], T.qw[:, 128 * k:128 * k + 128], T.sw[:, 128 * k:128 * k + 128],
             T.qf[:, a:b], T.sf[:, a:b], True, True))
 
     def own(q):
@@ -152,104 +169,129 @@ def rank_program(g, core, T, topo):
 
     def maps(q, i):
         a, b = 128 * PARTS[i][0], 128 * PARTS[i][1]
-        v = run(q, [lw[PARTS[i][0] // 4]], lambda e: e.quantize_mx(T.qw[:, a:b], T.sw[:, a:b], T.wt[:, 4 * a:4 * b]))
-        for k in range(*PARTS[i]):
-            got["M", k] = product(k, 0, COLS, [v, got["X",]])
-        return v
+        return run(q, lw[PARTS[i][0] // 4], lambda e: e.quantize_mx(T.qw[:, a:b], T.sw[:, a:b], T.wt[:, 4 * a:4 * b]))
 
-    def keep(q, dep, k, a, n, to):
-        return copy(q, [dep], T.win[:, k * WIN + to:k * WIN + to + n], T.ps[:, 512 * k + a:512 * k + a + n])
+    def part(k):
+        return ("W", [i for i, (a, b) in enumerate(PARTS) if a <= k < b][0])
 
-    early = [x[1] for q in "vs" for x in ORDER[q] if x[0] == "N"]
+    stages = sorted((x for q in "vs" for x in ORDER[q] if x[0] == "E"), key=lambda x: (x[3], x[1]))
+
+    order = list(ORDER.get("t") or [("A", k) for k in range(MAPS)] + [("A",) + x[1:] for x in stages])
+
+    def bank(k, *x):
+        return BANK.get((k,) + x, k)
+
+    def emptied(*x):
+        last = [y[1:] for y in order[:order.index(("A",) + x)] if bank(*y[1:]) == bank(*x)][-1:]
+        return [("E" if y[1:] else "O",) + y for y in last]
+
+    def times_own(q, k):
+        return product(k, k, 0, COLS, [got[part(k)], got["X",]] + [got[y] for y in emptied(k)])
+
+    def times_slots(q, k, lo, hi):
+        b = COLS + CAPP * hi
+        return product(k, bank(k, lo, hi), min(COLS + CAPP * lo, b - 128), b,
+                       [got[part(k)], got["X",]] + [got[y] for y in emptied(k, lo, hi)] + landed[max(0, min(lo, hi - 2)):hi])
 
     def keep_own(q, k):
-        return keep(q, got["M", k], k, 0, COLS, 1)
+        return copy(q, [got["A", k]], T.win[:, k * WIN + 1:k * WIN + 1 + COLS], T.ps[:, 512 * k:512 * k + COLS])
 
-    def keep_near(q, k):
-        for x in [x for x in early if x <= k and ("B", x) not in got]:
-            got["B", x] = product(x, COLS - pad, COLS + CAPP, [got["O", x], here])
-        return keep(q, got["B", k], k, pad, CAPP, 1 + COLS + CAPP * near)
+    def keep_slots(q, k, lo, hi):
+        runs, a = [], 512 * bank(k, lo, hi) + max(0, 128 - CAPP * (hi - lo))
+        for s in src[lo:hi]:
+            if runs and sum(runs[-1]) == s:
+                runs[-1][1] += 1
+            else:
+                runs.append([s, 1])
+        for s, n in runs:
+            to = k * WIN + 1 + COLS + CAPP * s
+            v = copy(q, [got["A", k, lo, hi]], T.win[:, to:to + CAPP * n], T.ps[:, a:a + CAPP * n])
+            a += CAPP * n
+        return v
 
-    def keep_far(q, k):
-        for x in [x for x in range(k + 1) if ("A", x) not in got]:
-            got["A", x] = product(x, COLS + CAPP * (x in early), COLS + SLOTS, [got["N" if x in early else "O", x], here, there])
-        if k in early:
-            return keep(q, got["A", k], k, 0, 2 * CAPP, 1 + COLS + CAPP * far[0])
-        if near + 1 == far[0]:
-            return keep(q, got["A", k], k, 0, SLOTS, 1 + COLS + CAPP * near)
-        keep(q, got["A", k], k, 0, CAPP, 1 + COLS + CAPP * near)
-        return keep(q, got["A", k], k, CAPP, 2 * CAPP, 1 + COLS + CAPP * far[0])
-
-    def terms(q, j):
-        return [x[1] for x in ORDER[q] if x[0] == "P" and x[2] <= j <= x[-1]]
+    def terms(j):
+        return [x[1] for q in "sv" for x in ORDER[q] if x[0] == "P" and x[2] <= j <= x[-1]]
 
     def pick(k, a, b):
         return T.win[:, k * WIN:k * WIN + WIN].indirect(T.mo[:, 32 * k + a // 16:32 * k + b // 16])
 
     def ready(k):
-        return base + [got["O", k], got["E", k]] + ([got["N", k]] if k in early else [])
-
-    def spot(i, a, b):
-        return T.pq[:, TERMS * a + i:TERMS * b:TERMS]
+        return base + [got["O", k]] + [got[x] for x in stages if x[1] == k]
 
     def before(k, j, a=0, b=16):
-        mine = terms("v", j)
-        i = mine.index(k) if k in mine else len(mine)
-        if k not in mine and j in SCANNED:
+        if j in SCANNED:
             return ("Z", j), T.zz[:, TERMS * a + TERMS - 1:TERMS * b:TERMS]
-        if i == 0:
-            return ("P", terms("s", j)[0], j), T.gs[:, a:b]
-        return ("P", mine[i - 1], j), T.vs[:, COLS * (i - 1) + a:COLS * (i - 1) + b]
+        i = (terms(j) + [k]).index(k)
+        return ("P", terms(j)[i - 1], j), T.vs[:, COLS * (i - 1) + a:COLS * (i - 1) + b]
 
-    def term(q, k, j, last=None):
-        js = range(j, (last or j) + 1)
+    def term(q, k, j, end=None):
+        js = range(j, (end or j) + 1)
         a, b = CUT[j][0], CUT[js[-1]][1]
-        mine = terms(q, j)
-        i = mine.index(k)
-        assert all(terms(q, x).index(k) == i for x in js)
-        if q == "s":
-            v = copy(q, ready(k), T.gs[:, a:b] if i == 0 and terms("v", j) else spot(i, a, b), pick(k, a, b))
+        i = terms(j).index(k)
+        assert all(terms(x).index(k) == i for x in js)
+        if j in SCANNED:
+            v = copy(q, ready(k), T.pq[:, TERMS * a + i:TERMS * b:TERMS], pick(k, a, b))
+        elif i == 0:
+            v = copy(q, ready(k), T.vs[:, a:b], pick(k, a, b))
         else:
-            o = spot(0, a, b) if j in SCANNED and i == len(mine) - 1 else T.vs[:, COLS * i + a:COLS * i + b]
-            v = run(q, ready(k) + [got[before(k, x)[0]] for x in js], lambda e: e.tensor_tensor(o, pick(k, a, b), before(k, j, a, b)[1], add))
+            v = run(q, ready(k) + [got[before(k, x)[0]] for x in js], lambda e: e.tensor_tensor(
+                T.vs[:, COLS * i + a:COLS * i + b], pick(k, a, b), before(k, j, a, b)[1], add))
         got.update({("P", k, x): v for x in js})
+        return v
+
+    def alone(q, k, j, end=None):
+        a, b = CUT[j][0], CUT[end or j][1]
+        v = copy(q, ready(k), T.bs[:, a:b], pick(k, a, b))
+        got["b"] = run("y", [v], lambda e: e.dma_start(T.y[:, a:b], T.bs[:, a:b]), "db", 16)
         return v
 
     def scan(q, j):
         a, b = TERMS * CUT[j][0], TERMS * CUT[j][1]
-        return run(q, [one] + [got["P", k, j] for k in terms("v", j) + terms("s", j)], lambda e: e.tensor_tensor_scan(
+        return run(q, [one] + [got["P", k, j] for k in terms(j)], lambda e: e.tensor_tensor_scan(
             T.zz[:, a:b], T.one[:, 0:b - a], T.pq[:, a:b], 0.0, AluOpType.mult, add))
 
-    def finish(q, k, j, last=None):
-        js = range(j, (last or j) + 1)
+    def finish(q, k, j, end=None):
+        js = range(j, (end or j) + 1)
         a, b = CUT[j][0], CUT[js[-1]][1]
         v = run(q, ready(k) + [got[before(k, x)[0]] for x in js], lambda e: e.tensor_tensor(
             T.ys[:, a:b], pick(k, a, b), before(k, j, a, b)[1], add))
-        got["y"] = run("y", [v], lambda e: e.dma_start(T.y[:, a:b], T.ys[:, a:b]), "dy", 16)
+        if js[-1] in HELD:
+            return v
+        while j - 1 in HELD:
+            j -= 1
+            a = CUT[j][0]
+        if j not in split:
+            got["y"] = run("y", [v], lambda e: e.dma_start(T.y[:, a:b], T.ys[:, a:b]), "dy", 16)
+        else:
+            got["a"] = run("g", [got["b"], v], lambda e: e.dma_start(T.y[:, a:b], T.ys[:, a:b], accum_op=add), "da", 16)
         return v
 
-    def needs(q, x):
+    def needs(x):
         if x[0] == "Q":
             return [("G", i, t) for i in range(x[1] + 1) for t in range(4)]
-        if x[0] == "O":
-            return [("W", i) for i, (a, b) in enumerate(PARTS) if a <= x[1] < b]
-        if x[0] == "N":
-            return [("W", len(PARTS) - 1)] + [("O", k) for k in early if k <= x[1]]
-        if x[0] == "E":
-            return [("O", k) for k in range(x[1] + 1)] + [("N", k) for k in early]
+        if x[0] == "A":
+            return emptied(*x[1:]) + [part(x[1]), ("X",)]
+        if x[0] in "OE":
+            return [("A",) + x[1:]]
         if x[0] == "Z":
-            return [("P", k, x[1]) for k in terms("v", x[1]) + terms("s", x[1])]
-        if x[0] in "PF":
-            return [("E", x[1])] + ([before(x[1], j)[0] for j in range(x[2], x[-1] + 1)] if q == "v" else [])
+            return [("P", k, x[1]) for k in terms(x[1])]
+        if x[0] in "BPF":
+            full = [("O", x[1])] + [y for y in stages if y[1] == x[1]]
+            if x[0] == "B" or x[0] == "P" and (x[2] in SCANNED or terms(x[2])[0] == x[1]):
+                return full
+            return full + [before(x[1], j)[0] for j in range(x[2], x[-1] + 1)] + (["b"] if x[0] == "F" and x[2] in split else []) + (
+                [x[:2] + (x[2] - 1,)] if x[0] == "F" and x[2] - 1 in HELD else [])
         return []
 
-    calls = {"G": gather, "Q": pack, "X": own, "W": maps, "O": keep_own, "N": keep_near, "E": keep_far, "P": term, "Z": scan, "F": finish}
-    todo = {q: list(ORDER[q]) for q in "sv"}
-    while todo["s"] or todo["v"]:
-        left = len(todo["s"]) + len(todo["v"])
-        for q in "sv":
-            while todo[q] and all(x in got for x in needs(q, todo[q][0])):
+    calls = {"G": gather, "Q": pack, "X": own, "W": maps, "O": keep_own, "E": keep_slots, "P": term, "B": alone, "Z": scan, "F": finish,
+             "A": lambda q, k, *x: times_slots(q, k, *x) if x else times_own(q, k)}
+    todo = {"s": list(ORDER["s"]), "v": list(ORDER["v"]), "t": list(order)}
+    while any(todo.values()):
+        left = sum(map(len, todo.values()))
+        for q in todo:
+            while todo[q] and all(x in got for x in needs(todo[q][0])):
                 x = todo[q].pop(0)
                 got[x] = calls[x[0]](q, *x[1:])
-        assert len(todo["s"]) + len(todo["v"]) < left
+        assert sum(map(len, todo.values())) < left
     wait("y", [got["y"]])
+    wait("g", [("gone", count["gone"])] + ([got["a"]] if split else []))

from concourse.bass import DstId, RemoteDMATransfer
from concourse.mybir import dt, AluOpType, ActivationFunctionType

COLS, MAPS, CAPP, N = 512, 8, 96, 4
SLOTS = (N - 1) * CAPP
WIN = 1 + COLS + N * CAPP
PARTS = [(0, 1), (1, 2), (2, 4), (4, 6), (6, 8)]
BATCH = [(0, 96), (96, 192), (192, 288)]
SENDS = [[(True, [(0, 0, 96)]), (False, [(0, 0, 96)])], [(True, [(1, 96, 192)])], [(True, [(2, 192, 288)]), (False, [(1, 96, 192), (2, 192, 288)])]]
CUT = [(0, 192), (192, 352), (352, 448), (448, 512)]
STAGES = [2]
HELD = [2]
BANK = {(0, 0, 2): 3, (1, 0, 2): 4}
SCANNED = [2, 3]
TERMS = 7
FILLED = 1
ORDER = {
    "v": [("G", 0, 0), ("G", 0, 2), ("G", 2, 0), ("Q", 0), ("X",), ("W", 0), ("W", 1), ("Q", 1), ("W", 2), ("Q", 2), ("W", 3), ("W", 4)]
    + [("O", k) for k in (3, 5, 7)] + [("E", 0, 0, 2), ("E", 1, 0, 2), ("E", 1, 2, 3), ("E", 2, 0, 3)]
    + [x for a, b in zip((1, 2, 3, 4, 5), (1, 3, 4, 5, 6)) for x in (("P", a, 1), ("P", b, 0))]
    + [("P", 6, 1), ("F", 7, 0), ("F", 7, 1), ("Z", 2), ("Z", 3), ("F", 7, 2), ("F", 7, 3)],
    "s": [("G", 0, 1), ("G", 0, 3)] + [("G", 1, t) for t in range(4)] + [("G", 2, t) for t in (1, 2, 3)]
    + [("O", k) for k in (0, 1, 2, 4, 6)]
    + [("E", 0, 2, 3), ("P", 0, 1), ("P", 0, 0), ("E", 3, 0, 3), ("E", 4, 0, 3), ("B", 2, 0), ("E", 5, 0, 3), ("E", 6, 0, 3)]
    + [("P", 0, 2, 3), ("E", 7, 0, 3), ("P", 1, 2, 3)] + [("P", k, j) for j in (2, 3) for k in range(2, 7)],
    "t": [("A", k) for k in (0, 1, 2, 3, 4, 5, 7, 6)] + [("A", k, a, b) for a, b in ((0, 2), (2, 3)) for k in (0, 1)]
    + [("A", k, 0, 3) for k in range(2, MAPS)],
}

SCRATCH = {
    "xs": ("sbuf", [128, 4 * COLS], "bfloat16"),
    "wt": ("sbuf", [128, 512 * MAPS], "bfloat16"),
    "sl": ("sbuf", [32, N * CAPP // 16], "int32"),
    "so": ("sbuf", [128, N * CAPP // 16], "uint16"),
    "ml": ("sbuf", [16, MAPS * COLS // 16], "int32"),
    "mo": ("sbuf", [128, MAPS * COLS // 16], "uint16"),
    "h": ("sbuf", [128, 4 * (128 + SLOTS)], "bfloat16"),
    "hq": ("sbuf", [128, 128 * 6], "float8_e4m3fn_x4"),
    "hs": ("sbuf", [128, 128 * 6], "uint8"),
    "qf": ("sbuf", [128, COLS + SLOTS], "float8_e4m3fn_x4"),
    "sf": ("sbuf", [128, COLS + SLOTS], "uint8"),
    "qw": ("sbuf", [128, 128 * MAPS], "float8_e4m3fn_x4"),
    "sw": ("sbuf", [128, 128 * MAPS], "uint8"),
    "win": ("sbuf", [128, MAPS * WIN], "float32"),
    "vs": ("sbuf", [128, MAPS * COLS], "float32"),
    "bs": ("sbuf", [128, COLS], "float32"),
    "pq": ("sbuf", [128, MAPS * COLS], "float32"),
    "zz": ("sbuf", [128, MAPS * COLS], "float32"),
    "ys": ("sbuf", [128, COLS], "float32"),
    "one": ("sbuf", [128, MAPS * 256], "bfloat16"),
    "ps": ("psum", [128, 512 * MAPS], "float32"),
}
SEMAPHORES = ["v", "s", "t", "dx", "dl", "dw0", "dw1", "dm", "dr", "dg", "db", "dy", "da", "in0", "in1", "in2", "gone"]


def rank_program(g, core, T, topo):
    r = T.rank_of(core)
    if r is None:
        return
    cores = list(T.cores)

    def dests(s):
        others = [d for d in range(N) if d != s]
        return sorted(others, key=lambda d: (cores[d] in topo.cores_of(cores[s]), topo.die(cores[d]) == topo.die(cores[s])))

    def sources(d):
        return sorted((s for s in range(N) if s != d), key=lambda s: min((dests(s).index(d) + 1) % (N - 1), STAGES[0]))

    dest, src = dests(r), sources(r)
    Copy, add = ActivationFunctionType.Copy, AluOpType.add
    pad, c = max(CAPP // 4, 128 - BATCH[0][1]), CAPP // 16

    queue = {"v": g.vector, "s": g.scalar, "t": g.tensor, "y": g.sync, "g": g}
    count, seen, got = {}, {}, {}

    def wait(q, deps):
        for sem, n in deps:
            if seen.get((q, sem), 0) < n:
                queue[q].wait_ge(T.sem[sem], n)
                seen[(q, sem)] = n

    def run(q, deps, call, sem=None, n=1):
        wait(q, deps)
        sem = sem or q
        call(queue[q]).then_inc(T.sem[sem], n)
        count[sem] = count.get(sem, 0) + n
        return (sem, count[sem])

    def copy(q, deps, o, i):
        if q == "v":
            return run("v", deps, lambda e: e.tensor_copy(o, i))
        return run("s", deps, lambda e: e.activation(o, i, Copy))

    split = [j for x in ORDER["s"] if x[0] == "B" for j in x[2:]]

    lm = run("s", [], lambda q: q.dma_start(T.ml[:], T.mp[:]), "dm", 16)
    run("y", [], lambda q: q.dma_start(T.xs[0:32, :], T.x[0:32, :]), "dx", 16)
    for q, p in (("s", 0), ("y", 16)):
        ll = run(q, [], lambda e: e.dma_start(T.sl[p:p + 16, :], T.send[:]), "dl", 16)
    lx = run("y", [], lambda q: q.dma_start(T.xs[32:128, :], T.x[32:128, :]), "dx", 16)
    lw = [run(q, [], lambda e: e.dma_start(T.wt[p:z, a:a + 2048], T.w[p:z, a:a + 2048]), sem, 16)
          for q, sem, a, p, z in (("y", "dw0", 0, 0, 128), ("y", "dw1", 2048, 0, 112), ("g", "dg", 2048, 112, 128))]
    lw = [lw[:1], lw[1:]]

    h0 = run("v", [], lambda q: q.memset(T.h[:, 0:4 * pad], 0.0))
    base = [run("v", [], lambda q: q.memset(T.win[:, 0:MAPS * WIN:WIN], 0.0))]
    for k in range(MAPS):
        a = k * WIN + 1 + COLS + CAPP * r
        if k < FILLED:
            base.append(run("v", [], lambda q: q.memset(T.win[:, a:a + CAPP], 0.0)))
        else:
            base.append(copy("s", [h0], T.win[:, a:a + CAPP], T.h[:, 0:CAPP]))
    n = TERMS * max(CUT[j][1] - CUT[j][0] for j in SCANNED)
    one = run("v", [], lambda q: q.memset(T.one[:, 0:n], 1.0))
    one = run("v", [one], lambda q: q.memset(T.one[:, 0:n:TERMS], 0.0))
    mo = run("v", [lm], lambda q: q.tensor_scalar(T.mo[0:16, :], T.ml[:], 1.0, None, add))
    for p in range(16, 128, 16):
        mr = run("y", [mo], lambda q: q.dma_start(T.mo[p:p + 16, :], T.mo[0:16, :]), "dr", 16)
    base += [mo, mr]
    for p in range(0, 128, 32):
        so = run("v", [ll], lambda q: q.tensor_scalar(T.so[p:p + 32, :], T.sl[:], 0.0, 4.0, AluOpType.max, AluOpType.mult))

    off = topo.engines(core, cores[dest[0]])
    on = [e for e in topo.engines(core, cores[dest[-1]]) if e not in off]

    def engines(x, which):
        far = [y for y in which if y[1] // CAPP != N - 2]
        return off[far.index(x)::len(far)] if x in far else on

    landed = [("in%d" % u, sum(len(engines(x, w)) for y in SENDS for _, w in y for x in w if (x[1] // CAPP + 1) % (N - 1) == u))
              for u in range(N - 1)]

    def send(codes, which):
        out = []
        for i, lo, hi in which:
            u, e = lo // CAPP, engines((i, lo, hi), which)
            rid, pid = topo.addr(cores[dest[u]], core)
            a, b, n = 192 * (i + 1) - BATCH[i][1] + lo, COLS + CAPP * sources(dest[u]).index(r) + lo % CAPP, hi - lo
            if codes:
                a, b = T.hq[:, a:a + n].bitcast(dt.uint8), T.qf[:, b:b + n].bitcast(dt.uint8)
            else:
                a, b = T.hs[:, a:a + n], T.sf[:, b:b + n]
            out.append(RemoteDMATransfer(srcs=[a], dsts=[b], dst_ids=[DstId(rid=rid, pnc=pid)], dma_engine_mask=sum(1 << x for x in e),
                                         remote_sem=T.sem[landed[(u + 1) % (N - 1)][0]]))
            count["gone"] = count.get("gone", 0) + len(e)
        g.remote_dma_fused(out, local_sem=T.sem.gone)

    def gather(q, i, t):
        a, b = BATCH[i]
        z = CAPP * (dest[a // CAPP] - a // CAPP) * (b - a <= CAPP)
        return copy(q, [so, lx], T.h[:, 4 * (pad + a) + t:4 * (pad + b):4], T.xs[:, t:4 * COLS].indirect(T.so[:, (a + z) // 16:(b + z) // 16]))

    def pack(q, i):
        a, b, n = 192 * (i + 1), pad + BATCH[i][1], max(128, BATCH[i][1] - BATCH[i][0])
        v = run(q, [h0] + [got["G", x, t] for x in range(i + 1) for t in range(4)], lambda e: e.quantize_mx(
            T.hq[:, a - n:a], T.hs[:, a - n:a], T.h[:, 4 * (b - n):4 * b]))
        wait("g", [v])
        for x in SENDS[i]:
            send(*x)
        return v

    def product(k, bank, a, b, deps):
        return run("t", deps, lambda q: q.matmul_mx(
            T.ps[:, 512 * bank:512 * bank + b - a], T.qw[:, 128 * k:128 * k + 128], T.sw[:, 128 * k:128 * k + 128],
            T.qf[:, a:b], T.sf[:, a:b], True, True))

    def own(q):
        return run(q, [lx], lambda e: e.quantize_mx(T.qf[:, 0:COLS], T.sf[:, 0:COLS], T.xs[:]))

    def maps(q, i):
        a, b = 128 * PARTS[i][0], 128 * PARTS[i][1]
        return run(q, lw[PARTS[i][0] // 4], lambda e: e.quantize_mx(T.qw[:, a:b], T.sw[:, a:b], T.wt[:, 4 * a:4 * b]))

    def part(k):
        return ("W", [i for i, (a, b) in enumerate(PARTS) if a <= k < b][0])

    stages = sorted((x for q in "vs" for x in ORDER[q] if x[0] == "E"), key=lambda x: (x[3], x[1]))

    order = list(ORDER.get("t") or [("A", k) for k in range(MAPS)] + [("A",) + x[1:] for x in stages])

    def bank(k, *x):
        return BANK.get((k,) + x, k)

    def emptied(*x):
        last = [y[1:] for y in order[:order.index(("A",) + x)] if bank(*y[1:]) == bank(*x)][-1:]
        return [("E" if y[1:] else "O",) + y for y in last]

    def times_own(q, k):
        return product(k, k, 0, COLS, [got[part(k)], got["X",]] + [got[y] for y in emptied(k)])

    def times_slots(q, k, lo, hi):
        b = COLS + CAPP * hi
        return product(k, bank(k, lo, hi), min(COLS + CAPP * lo, b - 128), b,
                       [got[part(k)], got["X",]] + [got[y] for y in emptied(k, lo, hi)] + landed[max(0, min(lo, hi - 2)):hi])

    def keep_own(q, k):
        return copy(q, [got["A", k]], T.win[:, k * WIN + 1:k * WIN + 1 + COLS], T.ps[:, 512 * k:512 * k + COLS])

    def keep_slots(q, k, lo, hi):
        runs, a = [], 512 * bank(k, lo, hi) + max(0, 128 - CAPP * (hi - lo))
        for s in src[lo:hi]:
            if runs and sum(runs[-1]) == s:
                runs[-1][1] += 1
            else:
                runs.append([s, 1])
        for s, n in runs:
            to = k * WIN + 1 + COLS + CAPP * s
            v = copy(q, [got["A", k, lo, hi]], T.win[:, to:to + CAPP * n], T.ps[:, a:a + CAPP * n])
            a += CAPP * n
        return v

    def terms(j):
        return [x[1] for q in "sv" for x in ORDER[q] if x[0] == "P" and x[2] <= j <= x[-1]]

    def pick(k, a, b):
        return T.win[:, k * WIN:k * WIN + WIN].indirect(T.mo[:, 32 * k + a // 16:32 * k + b // 16])

    def ready(k):
        return base + [got["O", k]] + [got[x] for x in stages if x[1] == k]

    def before(k, j, a=0, b=16):
        if j in SCANNED:
            return ("Z", j), T.zz[:, TERMS * a + TERMS - 1:TERMS * b:TERMS]
        i = (terms(j) + [k]).index(k)
        return ("P", terms(j)[i - 1], j), T.vs[:, COLS * (i - 1) + a:COLS * (i - 1) + b]

    def term(q, k, j, end=None):
        js = range(j, (end or j) + 1)
        a, b = CUT[j][0], CUT[js[-1]][1]
        i = terms(j).index(k)
        assert all(terms(x).index(k) == i for x in js)
        if j in SCANNED:
            v = copy(q, ready(k), T.pq[:, TERMS * a + i:TERMS * b:TERMS], pick(k, a, b))
        elif i == 0:
            v = copy(q, ready(k), T.vs[:, a:b], pick(k, a, b))
        else:
            v = run(q, ready(k) + [got[before(k, x)[0]] for x in js], lambda e: e.tensor_tensor(
                T.vs[:, COLS * i + a:COLS * i + b], pick(k, a, b), before(k, j, a, b)[1], add))
        got.update({("P", k, x): v for x in js})
        return v

    def alone(q, k, j, end=None):
        a, b = CUT[j][0], CUT[end or j][1]
        v = copy(q, ready(k), T.bs[:, a:b], pick(k, a, b))
        got["b"] = run("y", [v], lambda e: e.dma_start(T.y[:, a:b], T.bs[:, a:b]), "db", 16)
        return v

    def scan(q, j):
        a, b = TERMS * CUT[j][0], TERMS * CUT[j][1]
        return run(q, [one] + [got["P", k, j] for k in terms(j)], lambda e: e.tensor_tensor_scan(
            T.zz[:, a:b], T.one[:, 0:b - a], T.pq[:, a:b], 0.0, AluOpType.mult, add))

    def finish(q, k, j, end=None):
        js = range(j, (end or j) + 1)
        a, b = CUT[j][0], CUT[js[-1]][1]
        v = run(q, ready(k) + [got[before(k, x)[0]] for x in js], lambda e: e.tensor_tensor(
            T.ys[:, a:b], pick(k, a, b), before(k, j, a, b)[1], add))
        if js[-1] in HELD:
            return v
        while j - 1 in HELD:
            j -= 1
            a = CUT[j][0]
        if j not in split:
            got["y"] = run("y", [v], lambda e: e.dma_start(T.y[:, a:b], T.ys[:, a:b]), "dy", 16)
        else:
            got["a"] = run("g", [got["b"], v], lambda e: e.dma_start(T.y[:, a:b], T.ys[:, a:b], accum_op=add), "da", 16)
        return v

    def needs(x):
        if x[0] == "Q":
            return [("G", i, t) for i in range(x[1] + 1) for t in range(4)]
        if x[0] == "A":
            return emptied(*x[1:]) + [part(x[1]), ("X",)]
        if x[0] in "OE":
            return [("A",) + x[1:]]
        if x[0] == "Z":
            return [("P", k, x[1]) for k in terms(x[1])]
        if x[0] in "BPF":
            full = [("O", x[1])] + [y for y in stages if y[1] == x[1]]
            if x[0] == "B" or x[0] == "P" and (x[2] in SCANNED or terms(x[2])[0] == x[1]):
                return full
            return full + [before(x[1], j)[0] for j in range(x[2], x[-1] + 1)] + (["b"] if x[0] == "F" and x[2] in split else []) + (
                [x[:2] + (x[2] - 1,)] if x[0] == "F" and x[2] - 1 in HELD else [])
        return []

    calls = {"G": gather, "Q": pack, "X": own, "W": maps, "O": keep_own, "E": keep_slots, "P": term, "B": alone, "Z": scan, "F": finish,
             "A": lambda q, k, *x: times_slots(q, k, *x) if x else times_own(q, k)}
    todo = {"s": list(ORDER["s"]), "v": list(ORDER["v"]), "t": list(order)}
    while any(todo.values()):
        left = sum(map(len, todo.values()))
        for q in todo:
            while todo[q] and all(x in got for x in needs(todo[q][0])):
                x = todo[q].pop(0)
                got[x] = calls[x[0]](q, *x[1:])
        assert sum(map(len, todo.values())) < left
    wait("y", [got["y"]])
    wait("g", [("gone", count["gone"])] + ([got["a"]] if split else []))
